import numpy as np
import ml_dtypes


def mxq(x, axis, fmt="e4m3"):
    dtype, down = {"e4m3": (ml_dtypes.float8_e4m3fn, 7), "e5m2": (ml_dtypes.float8_e5m2, 14)}[fmt]
    v = np.moveaxis(np.asarray(x, np.float32).astype(ml_dtypes.bfloat16).astype(np.float64), axis, -1)
    blocks = v.reshape(v.shape[:-1] + (-1, 32))
    amax = np.abs(blocks).max(-1, keepdims=True)
    byte = np.maximum(np.where(amax > 0, np.frexp(amax)[1] - 1 + 127, 0) - down, 1)
    scale = np.exp2(byte - 127.0)
    codes = (blocks / scale).astype(np.float32).astype(dtype).astype(np.float64)
    return np.moveaxis((codes * scale).reshape(v.shape), -1, axis)


WIDE = False


def mx_kscale(k):
    if not WIDE:
        return np.ones(k)
    levels = np.array([10, -10, 5, -5, 0])
    if k % 512:
        return np.exp2(np.random.permutation(np.resize(levels, k // 32))).repeat(32)
    a = np.empty((k // 512, 16))
    for p in range(k // 512):
        a[p, :8] = np.random.permutation(np.resize(levels, 8))
        for g in range(8):
            far = levels[np.abs(levels - a[p, g]) >= 10]
            a[p, g + 8] = far[np.random.randint(len(far))]
    return np.exp2(a.ravel()).repeat(32)


BF16 = ml_dtypes.bfloat16


def bf(x):
    return np.asarray(x, np.float32).astype(BF16)


def f64(x):
    return np.asarray(x).astype(np.float64)


N, DA1, DV1, DT1, H, O = 8192, 16, 8, 4, 512, 256
DA, DV, DT = DA1 - 1, DV1 - 1, DT1 - 1
Z = DA1 * DV1 * DT1


def prepend_one(x):
    return np.concatenate([np.ones((x.shape[0], 1)), x], axis=-1)


def draw0():
    s, u = mx_kscale(Z), mx_kscale(H)
    return {"a": bf(np.random.standard_normal((N, DA))),
            "v": bf(np.random.standard_normal((N, DV))),
            "t": bf(np.random.standard_normal((N, DT))),
            "gz": bf((1.0 + 0.1 * np.random.standard_normal(Z)) * s),
            "w1": bf(np.random.standard_normal((Z, H)) / np.sqrt(Z) / s[:, None]),
            "gh": bf(np.random.standard_normal(H) * u),
            "w2": bf(1.4 * np.random.standard_normal((H, O)) / np.sqrt(H) / u[:, None])}


def core(a, v, t, gz, w1, gh, w2):
    a1 = prepend_one(f64(a))
    v1 = prepend_one(f64(v))
    t1 = prepend_one(f64(t))
    z4 = a1[:, :, None, None] * v1[:, None, :, None] * t1[:, None, None, :]
    z = z4.reshape(a.shape[0], w1.shape[0])
    zg = z * f64(gz)[None, :]
    p = mxq(zg, 1, "e4m3") @ mxq(f64(w1), 0, "e4m3")
    h = np.maximum(p, 0.0) * f64(gh)[None, :]
    return mxq(h, 1, "e4m3") @ mxq(f64(w2), 0, "e4m3")


def e4m3fn_bytes(y):
    return np.clip(np.asarray(y, np.float64), -448.0, 448.0).astype(np.float32).astype(ml_dtypes.float8_e4m3fn).view(np.uint8)


def e4m3fn_values(b):
    return np.asarray(b, np.uint8).view(ml_dtypes.float8_e4m3fn).astype(np.float64)


def setup_inputs():
    d = draw0()
    x0 = np.asarray(d['w1']).astype(np.float64)
    s = (np.max(np.abs(x0), axis=(1,), keepdims=True) / 448.0).astype(np.float32)
    out = {}
    for k, v in d.items():
        if k == 'w1':
            out['w1_bytes'] = e4m3fn_bytes(x0 / s.astype(np.float64))
            out['w1_scale'] = s
        else:
            out[k] = v
    return out


def reference(a, v, t, gz, w1_bytes, w1_scale, gh, w2):
    return core(a, v, t, gz, e4m3fn_values(w1_bytes) * w1_scale.astype(np.float64), gh, w2)

@@ -1,0 +1,368 @@
+from contextlib import ExitStack
+
+import concourse.mybir as mybir
+from concourse.masks import make_identity
+
+F32 = mybir.dt.float32
+BF16 = mybir.dt.bfloat16
+U32 = mybir.dt.uint32
+U8 = mybir.dt.uint8
+FP8 = mybir.dt.float8_e4m3fn
+FP8X4 = mybir.dt.float8_e4m3fn_x4
+ALU = mybir.AluOpType
+ACT = mybir.ActivationFunctionType
+
+N, DA, DV, DT, Z, H, O = 8192, 15, 7, 3, 512, 512, 256
+P = 128
+QS = N // P
+NCH = 16
+QC = QS // NCH
+CW = QC * P
+EARLY = 2
+CTYPE = 4
+ILV = 320
+FLOPS = 2 * N * Z * H + 2 * N * H * O
+
+
+def tile_tensorfusionouterproducthead_t_kernel(tc, a, v, t, gz, w1_bytes, w1_scale, gh, w2, out):
+    nc = tc.nc
+    with ExitStack() as ctx:
+        keep = ctx.enter_context(tc.tile_pool(name="keep", bufs=1))
+        work = ctx.enter_context(tc.tile_pool(name="work", bufs=2))
+        psum = ctx.enter_context(tc.psum_pool(name="psum", bufs=1))
+        ctx.enter_context(tc.manual_schedule())
+
+        t_nat = keep.tile([P, QS, DT], BF16)
+        v_nat = keep.tile([P, QS, DV], BF16)
+        a_nat = keep.tile([P, QS, DA], BF16)
+        gz_col = keep.tile([P, 4], BF16)
+        gz_row = keep.tile([P, Z], BF16)
+        gh_col = keep.tile([P, 4], BF16)
+        w1_raw = keep.tile([P, 4, H], U8)
+        w1_sc = keep.tile([P, 4], F32)
+        w2_raw = keep.tile([P, 4, O], BF16)
+        nc.sync.dma_start(out=a_nat[:], in_=a.rearrange("(h q) c -> h q c", q=QS))
+        nc.sync.dma_start(out=v_nat[:], in_=v.rearrange("(h q) c -> h q c", q=QS))
+        nc.sync.dma_start(out=t_nat[:], in_=t.rearrange("(h q) c -> h q c", q=QS))
+        nc.sync.dma_start(out=gz_col[:], in_=gz.rearrange("(p j) -> p j", j=4))
+        nc.sync.dma_start(out=w1_sc[:], in_=w1_scale.rearrange("(p j) o -> p (j o)", j=4))
+        nc.sync.dma_start(out=w1_raw[:], in_=w1_bytes.rearrange("(p j) n -> p j n", j=4))
+        nc.sync.dma_start(out=gh_col[:], in_=gh.rearrange("(p j) -> p j", j=4))
+        nc.sync.dma_start(out=w2_raw[:], in_=w2.rearrange("(p j) n -> p j n", j=4))
+        nc.sync.dma_start(out=gz_row[:], in_=gz.partition_broadcast(P))
+
+        ident = keep.tile([P, P], BF16)
+        make_identity(nc, ident[:])
+        a_mat = keep.tile([P, EARLY * QC, 16, 8], BF16)
+        v_mat = keep.tile([P, EARLY * QC, 16, 8], BF16)
+        a_pad = keep.tile([P, 16, QS], BF16)
+        v_pad = keep.tile([P, 8, QS], BF16)
+        t_pad = keep.tile([P, 4, QS], BF16)
+        sel = keep.tile([P, 4, P], BF16)
+        ones = keep.tile([P, CW], BF16)
+        nc.gpsimd.memset(ones[:], 1.0)
+        warm = keep.tile([P, 1], F32)
+        nc.vector.memset(warm[:], 0.0)
+        nc.vector.memset(a_mat[:], 1.0)
+        nc.gpsimd.memset(v_mat[:], 1.0)
+        nc.gpsimd.memset(a_pad[:, 0, :], 1.0)
+        nc.gpsimd.memset(v_pad[:, 0, :], 1.0)
+        nc.gpsimd.memset(t_pad[:, 0, :], 1.0)
+        nc.gpsimd.memset(sel[:], 0.0)
+        warm2 = keep.tile([P, 1], F32)
+        nc.scalar.activation(out=warm2[:], in_=warm[:], func=ACT.Relu)
+
+        ne = EARLY * QC
+        nc.vector.tensor_copy(
+            out=a_mat[:, :, 1:16, :],
+            in_=a_nat[:, 0:ne, :].unsqueeze(3).to_broadcast([P, ne, DA, 8]),
+        )
+        nc.scalar.copy(
+            out=v_mat[:, :, :, 1:8],
+            in_=v_nat[:, 0:ne, :].unsqueeze(2).to_broadcast([P, ne, 16, DV]),
+        )
+        gz_f = keep.tile([P, 4], F32)
+        nc.gpsimd.tensor_copy(out=gz_f[:], in_=gz_col[:])
+        nc.vector.tensor_copy(out=a_pad[:, 1:16, :], in_=a_nat[:].rearrange("p q c -> p c q"))
+        nc.gpsimd.tensor_copy(out=v_pad[:, 1:8, :], in_=v_nat[:].rearrange("p q c -> p c q"))
+        nc.gpsimd.tensor_copy(out=t_pad[:, 1:4, :], in_=t_nat[:].rearrange("p q c -> p c q"))
+        sgn01 = keep.tile([P, 4], BF16)
+        sgn = keep.tile([P, 4], BF16)
+        gh_abs = keep.tile([P, 4], F32)
+        nc.gpsimd.tensor_scalar(out=sgn01[:], in0=gh_col[:], scalar1=0.0, scalar2=None, op0=ALU.is_ge)
+        nc.gpsimd.tensor_scalar(out=sgn[:], in0=sgn01[:], scalar1=2.0, scalar2=-1.0, op0=ALU.mult, op1=ALU.add)
+        nc.gpsimd.tensor_tensor(out=gh_abs[:], in0=gh_col[:], in1=sgn[:], op=ALU.mult)
+        for k in range(4):
+            nc.gpsimd.tensor_copy(
+                out=sel[32 * k : 32 * k + 1, k, :],
+                in_=gz_row[32 * k : 32 * k + 1, :].rearrange("o (p j) -> o j p", j=4)[:, k, :],
+            )
+
+        tg = []
+        for i in range(2):
+            tgi = keep.tile([P, 4, CW], F32, name="tg%d" % i)
+            tg.append(tgi)
+        av_tiles = {}
+        y_tiles = []
+        zg_tiles = {}
+        zc_tiles = {}
+        hp_tiles = {}
+        hi_tiles = {}
+        hc_tiles = {}
+        pieces = {}
+        p1_tiles = {}
+
+        def early_factors(c):
+            a_ps = psum.tile([P, QC, P], BF16, name="a_ps", tag="p", bufs=3)
+            v_ps = psum.tile([P, QC, P], BF16, name="v_ps", tag="o", bufs=2)
+            for j in range(QC):
+                nc.tensor.transpose(v_ps[:, j, :], v_mat[:, QC * c + j].rearrange("p i s -> p (i s)"), ident[:])
+            for j in range(QC):
+                nc.tensor.transpose(a_ps[:, j, :], a_mat[:, QC * c + j].rearrange("p i s -> p (i s)"), ident[:])
+            v_sb = work.tile([P, CW], BF16, name="v_sb", tag="v_sb", bufs=2)
+            nc.scalar.copy(out=v_sb[:], in_=v_ps[:].rearrange("p q h -> p (q h)"))
+            av = work.tile([P, CW], F32, name="av", tag="av", bufs=3)
+            nc.vector.tensor_tensor(out=av[:], in0=a_ps[:].rearrange("p q h -> p (q h)"), in1=v_sb[:], op=ALU.mult)
+            av_tiles[c] = av
+
+        def late_factors(c):
+            ar, vr, r, base = pieces[c]
+            lo = c * CW - base
+            av = work.tile([P, CW], F32, name="av", tag="av", bufs=3)
+            nc.vector.tensor_tensor(out=av[:], in0=ar[:, lo : lo + CW], in1=vr[:, lo : lo + CW], op=ALU.mult)
+            av_tiles[c] = av
+
+        def t_planes(c):
+            tb0 = psum.tile([P, 2, CW], BF16, name="tb0", tag="y0", bufs=1)
+            tb1 = psum.tile([P, CW], BF16, name="tb1", tag="y1", bufs=1)
+            for k in range(DT):
+                for j in range(QC):
+                    q = QC * c + j
+                    dst = tb0[:, k, j * P : (j + 1) * P] if k < 2 else tb1[:, j * P : (j + 1) * P]
+                    nc.tensor.transpose(dst, t_nat[:, q, k : k + 1].to_broadcast([P, P]), ident[:])
+            for k in range(DT):
+                src = tb0[:, k, :] if k < 2 else tb1[:]
+                nc.scalar.activation(out=tg[c % 2][:, k + 1, :], in_=src, func=ACT.Copy, scale=gz_f[:, k + 1 : k + 2])
+
+        def y_block(c, j):
+            ar, vr, r, base = pieces[c]
+            lo = c * CW - base + j * P
+            y = y_tiles[(QC * c + j) % 3]
+            for k in range(1, 4):
+                nc.tensor.matmul(y[:, k, :], lhsT=sel[:, k, :], rhs=r[:, lo : lo + P], start=True, stop=True)
+
+        def fuse(c, j):
+            if j == 0:
+                zg = work.tile([P, CW, 4], BF16, name="zg", tag="zg", bufs=2, align_bytes=64)
+                zg_tiles[c] = zg
+            cols = slice(j * P, (j + 1) * P)
+            x = av_tiles[c][:, cols].unsqueeze(2).to_broadcast([P, P, 4])
+            if c < CTYPE:
+                y = tg[c % 2][:, :, cols]
+            else:
+                y = y_tiles[(QC * c + j) % 3][:]
+            nc.vector.tensor_tensor(out=zg_tiles[c][:, cols, :], in0=y.rearrange("p k n -> p n k"), in1=x, op=ALU.mult)
+
+        def quant_z(c):
+            zc = work.tile([P, CW], U32, name="zc", tag="zc", bufs=2, align_bytes=64)
+            zs = work.tile([P, CW], U8, name="zs", tag="zs", bufs=2, align_bytes=64)
+            nc.vector.quantize_mx(out=zc[:].bitcast(FP8X4), scales=zs[:], in_=zg_tiles[c][:].rearrange("p n k -> p (n k)"))
+            zc_tiles[c] = (zc, zs)
+
+        def stage1(c, ks, vec_ks=()):
+            zc, zs = zc_tiles[c]
+            if c not in hp_tiles:
+                hp = work.tile([P, 4, CW], BF16, name="hp", tag="hp", bufs=2)
+                hp_tiles[c] = hp
+            hp = hp_tiles[c]
+            for k in ks:
+                p1 = psum.tile([P, CW], F32, name="p1", tag="p", bufs=3)
+                nc.tensor.matmul_mx(
+                    out=p1[:],
+                    lhsT=w1_codes[:, k * P : (k + 1) * P].bitcast(FP8X4),
+                    lhsT_scale=w1_scales[:, k * P : (k + 1) * P],
+                    rhs=zc[:].bitcast(FP8X4),
+                    rhs_scale=zs[:],
+                    start=True,
+                    stop=True,
+                )
+                p1_tiles[c, k] = p1
+                if k not in vec_ks:
+                    nc.scalar.activation(out=hp[:, k, :], in_=p1[:], func=ACT.Relu, scale=gh_abs[:, k : k + 1])
+
+        def relu_v(c, k):
+            nc.vector.tensor_scalar(out=hp_tiles[c][:, k, :], in0=p1_tiles[c, k][:], scalar1=0.0, scalar2=gh_abs[:, k : k + 1],
+                                    op0=ALU.max, op1=ALU.mult)
+
+        def interleave(eng, c, lo, hi):
+            if c not in hi_tiles:
+                ht = work.tile([P, CW, 4], BF16, name="ht", tag="ht", bufs=2, align_bytes=64)
+                hi_tiles[c] = ht
+            dst = hi_tiles[c][:, lo:hi, :].rearrange("p (c i) k -> p c k i", i=4)
+            src = hp_tiles[c][:, :, lo:hi].rearrange("p k (c i) -> p c k i", i=4)
+            if eng == "v":
+                nc.vector.tensor_copy(out=dst, in_=src)
+            else:
+                nc.scalar.copy(out=dst, in_=src)
+
+        def quant_h(c, lo=0, hi=CW):
+            if c not in hc_tiles:
+                hc = work.tile([P, CW], U32, name="hc", tag="hc", bufs=2, align_bytes=64)
+                hs = work.tile([P, CW], U8, name="hs", tag="hs", bufs=2, align_bytes=64)
+                hc_tiles[c] = (hc, hs)
+            hc, hs = hc_tiles[c]
+            nc.vector.quantize_mx(out=hc[:, lo:hi].bitcast(FP8X4), scales=hs[:, lo:hi],
+                                  in_=hi_tiles[c][:, lo:hi, :].rearrange("p n k -> p (n k)"))
+
+        out_v = out.rearrange("(h q) o -> h q o", q=QS)
+        o_tiles = {}
+
+        def stage2(c, jj, vec=False, store=None):
+            hc, hs = hc_tiles[c]
+            if c not in o_tiles:
+                osb = work.tile([P, QC, O], F32, name="osb", tag="osb", bufs=3)
+                o_tiles[c] = osb
+            osb = o_tiles[c]
+            po = psum.tile([P, 2, O], F32, name="po", tag="o", bufs=2)
+            for j in range(2):
+                cols = slice((2 * jj + j) * P, (2 * jj + j + 1) * P)
+                nc.tensor.matmul_mx(
+                    out=po[:, j, :],
+                    lhsT=hc[:, cols].bitcast(FP8X4),
+                    lhsT_scale=hs[:, cols],
+                    rhs=w2_codes[:].bitcast(FP8X4),
+                    rhs_scale=w2_scales[:],
+                    start=True,
+                    stop=True,
+                )
+            if vec:
+                nc.vector.tensor_copy(out=osb[:, 2 * jj : 2 * jj + 2, :], in_=po[:])
+            else:
+                nc.scalar.copy(out=osb[:, 2 * jj : 2 * jj + 2, :], in_=po[:])
+            if store is not None:
+                nc.sync.dma_start(out=out_v[:, QC * c + store[0] : QC * c + store[1], :], in_=osb[:, store[0] : store[1], :])
+
+        early_factors(0)
+        t_planes(0)
+        for i in range(2):
+            nc.vector.tensor_scalar(out=tg[i][:, 0, :], in0=ones[:], scalar1=gz_f[:, 0:1], scalar2=None, op0=ALU.mult)
+        turned = keep.tile([P, 14, P], BF16)
+        src_cols = [a_pad[:].rearrange("p c q -> p (c q)"), v_pad[:].rearrange("p c q -> p (c q)"), t_pad[:].rearrange("p c q -> p (c q)")]
+        m = 0
+        for cols_ap, cnt in ((src_cols[0], 4), (src_cols[0], 4), (src_cols[1], 4), (src_cols[2], 2)):
+            first = 4 if m == 4 else 0
+            tp = psum.tile([P, 4, P], BF16, name="tp", tag="p", bufs=3)
+            for i in range(cnt):
+                nc.tensor.transpose(tp[:, i, :], cols_ap[:, (first + i) * P : (first + i + 1) * P], ident[:])
+            nc.scalar.copy(out=turned[:, m : m + cnt, :], in_=tp[:, 0:cnt, :])
+            m += cnt
+        park_rows = 14 * P * P // 2 // O
+        park = out[N - park_rows : N, :].rearrange("r o -> (r o)").bitcast(BF16)
+        nc.sync.dma_start(out=park.rearrange("(m p h) -> p m h", p=P, h=P), in_=turned[:])
+        a_park = park[0 : 16 * N].rearrange("(i n) -> i n", i=16)
+        for c0, c1 in ((2, 4), (4, 8), (8, 16)):
+            n0, n1 = c0 * CW, c1 * CW
+            w = n1 - n0
+            ar = keep.tile([P, w], BF16, name="ar%d" % c0)
+            vr = keep.tile([P, w], BF16, name="vr%d" % c0)
+            r = None
+            for s in range(8):
+                nc.sync.dma_start(out=ar[s:P:8, :], in_=a_park[:, n0:n1])
+            for s in range(8):
+                nc.sync.dma_start(out=vr[s:P:8, :], in_=park[(16 + s) * N + n0 : (16 + s) * N + n1].partition_broadcast(16))
+            if c0 >= CTYPE:
+                r = keep.tile([P, w], BF16, name="r%d" % c0)
+                for k in range(4):
+                    nc.sync.dma_start(out=r[32 * k : 32 * k + 32, :], in_=park[(24 + k) * N + n0 : (24 + k) * N + n1].partition_broadcast(32))
+            for c in range(c0, c1):
+                pieces[c] = (ar, vr, r, n0)
+
+        w1_wide = keep.tile([P, 4, H], BF16)
+        w1_grp = keep.tile([P, H, 4], BF16, align_bytes=64)
+        w1_codes = keep.tile([P, H], U32, align_bytes=64)
+        w1_scales = keep.tile([P, H], U8, align_bytes=64)
+        w2_grp = keep.tile([P, O, 4], BF16, align_bytes=64)
+        w2_codes = keep.tile([P, O], U32, align_bytes=64)
+        w2_scales = keep.tile([P, O], U8, align_bytes=64)
+        for k in range(4):
+            nc.scalar.activation(out=w1_wide[:, k, :], in_=w1_raw[:, k, :].bitcast(FP8), func=ACT.Copy, scale=w1_sc[:, k : k + 1])
+
+        def weights1():
+            nc.vector.tensor_copy(
+                out=w1_grp[:].rearrange("p (k m) j -> p k m j", k=4),
+                in_=w1_wide[:].rearrange("p j (m k) -> p k m j", k=4),
+            )
+
+        def weights2():
+            nc.vector.tensor_tensor(
+                out=w2_grp[:],
+                in0=w2_raw[:].rearrange("p j n -> p n j"),
+                in1=sgn[:].unsqueeze(1).to_broadcast([P, O, 4]),
+                op=ALU.mult,
+            )
+            nc.vector.quantize_mx(out=w1_codes[:].bitcast(FP8X4), scales=w1_scales[:], in_=w1_grp[:].rearrange("p n j -> p (n j)"))
+
+        def weights3():
+            nc.vector.quantize_mx(out=w2_codes[:].bitcast(FP8X4), scales=w2_scales[:], in_=w2_grp[:].rearrange("p n j -> p (n j)"))
+
+        for r in range(NCH):
+            if r >= 1:
+                fuse(r - 1, 3)
+            if CTYPE <= r:
+                y_block(r, 2)
+            for j in range(3):
+                fuse(r, j)
+            if r == 0:
+                weights1()
+            if r + 1 < NCH:
+                if r + 1 < EARLY:
+                    early_factors(r + 1)
+                else:
+                    late_factors(r + 1)
+                if r + 1 < CTYPE:
+                    t_planes(r + 1)
+            if r == CTYPE - 1:
+                for i in range(3):
+                    y = psum.tile([P, 4, P], F32, name="y%d" % i, tag="y%d" % i, bufs=1)
+                    nc.tensor.matmul(y[:, 0, :], lhsT=sel[:, 0, :], rhs=pieces[CTYPE][2][:, 0:P], start=True, stop=True)
+                    y_tiles.append(y)
+            if CTYPE <= r:
+                y_block(r, 3)
+            if CTYPE <= r + 1 < NCH:
+                y_block(r + 1, 0)
+                y_block(r + 1, 1)
+            if r == 0:
+                weights2()
+            if 0 <= r - 2 < NCH - 2:
+                interleave("s", r - 2, ILV, CW)
+            if 0 <= r - 3 < NCH - 3:
+                quant_h(r - 3)
+                stage2(r - 3, 0)
+                stage2(r - 3, 1, store=(0, 4))
+            if 0 <= r - 1 < NCH - 1:
+                quant_z(r - 1)
+                stage1(r - 1, range(4))
+            if r == 0:
+                weights3()
+            if 0 <= r - 2 < NCH - 2:
+                interleave("v", r - 2, 0, ILV)
+        last = NCH - 1
+        fuse(last, 3)
+        quant_z(last)
+        stage1(last, (0, 1, 2), (2,))
+        quant_h(last - 2)
+        stage2(last - 2, 0)
+        stage2(last - 2, 1, store=(0, 4))
+        stage1(last, (3,), (3,))
+        interleave("v", last - 1, 0, CW)
+        relu_v(last, 2)
+        relu_v(last, 3)
+        quant_h(last - 1)
+        stage2(last - 1, 0)
+        interleave("v", last, 0, CW // 2)
+        stage2(last - 1, 1, store=(0, 4))
+        interleave("v", last, CW // 2, CW)
+        quant_h(last, 0, CW // 2)
+        stage2(last, 0, store=(0, 2))
+        quant_h(last, CW // 2, CW)
+        stage2(last, 1, vec=True, store=(2, 4))

@@ -18,9 +18,12 @@ QS = N // P
 NCH = 16
 QC = QS // NCH
 CW = QC * P
-EARLY = 2
+EARLY = 4
 CTYPE = 4
-ILV = 320
+ILG = 192
+ILV = 400
+AVB = 2
+PB = 3
 FLOPS = 2 * N * Z * H + 2 * N * H * O
 
 
@@ -41,10 +44,10 @@ def tile_tensorfusionouterproducthead_t_kernel(tc, a, v, t, gz, w1_bytes, w1_sca
         w1_raw = keep.tile([P, 4, H], U8)
         w1_sc = keep.tile([P, 4], F32)
         w2_raw = keep.tile([P, 4, O], BF16)
-        nc.sync.dma_start(out=a_nat[:], in_=a.rearrange("(h q) c -> h q c", q=QS))
-        nc.sync.dma_start(out=v_nat[:], in_=v.rearrange("(h q) c -> h q c", q=QS))
         nc.sync.dma_start(out=t_nat[:], in_=t.rearrange("(h q) c -> h q c", q=QS))
         nc.sync.dma_start(out=gz_col[:], in_=gz.rearrange("(p j) -> p j", j=4))
+        nc.sync.dma_start(out=v_nat[:], in_=v.rearrange("(h q) c -> h q c", q=QS))
+        nc.sync.dma_start(out=a_nat[:], in_=a.rearrange("(h q) c -> h q c", q=QS))
         nc.sync.dma_start(out=w1_sc[:], in_=w1_scale.rearrange("(p j) o -> p (j o)", j=4))
         nc.sync.dma_start(out=w1_raw[:], in_=w1_bytes.rearrange("(p j) n -> p j n", j=4))
         nc.sync.dma_start(out=gh_col[:], in_=gh.rearrange("(p j) -> p j", j=4))
@@ -53,55 +56,66 @@ def tile_tensorfusionouterproducthead_t_kernel(tc, a, v, t, gz, w1_bytes, w1_sca
 
         ident = keep.tile([P, P], BF16)
         make_identity(nc, ident[:])
-        a_mat = keep.tile([P, EARLY * QC, 16, 8], BF16)
-        v_mat = keep.tile([P, EARLY * QC, 16, 8], BF16)
+        a_mats = []
+        v_mats = []
+        for c in range(EARLY):
+            am = keep.tile([P, QC, 16, 8], BF16, name="a_mat%d" % c)
+            vm = keep.tile([P, QC, 16, 8], BF16, name="v_mat%d" % c)
+            a_mats.append(am)
+            v_mats.append(vm)
         a_pad = keep.tile([P, 16, QS], BF16)
         v_pad = keep.tile([P, 8, QS], BF16)
         t_pad = keep.tile([P, 4, QS], BF16)
         sel = keep.tile([P, 4, P], BF16)
         ones = keep.tile([P, CW], BF16)
-        nc.gpsimd.memset(ones[:], 1.0)
         warm = keep.tile([P, 1], F32)
-        nc.vector.memset(warm[:], 0.0)
-        nc.vector.memset(a_mat[:], 1.0)
-        nc.gpsimd.memset(v_mat[:], 1.0)
-        nc.gpsimd.memset(a_pad[:, 0, :], 1.0)
-        nc.gpsimd.memset(v_pad[:, 0, :], 1.0)
-        nc.gpsimd.memset(t_pad[:, 0, :], 1.0)
-        nc.gpsimd.memset(sel[:], 0.0)
         warm2 = keep.tile([P, 1], F32)
-        nc.scalar.activation(out=warm2[:], in_=warm[:], func=ACT.Relu)
-
-        ne = EARLY * QC
-        nc.vector.tensor_copy(
-            out=a_mat[:, :, 1:16, :],
-            in_=a_nat[:, 0:ne, :].unsqueeze(3).to_broadcast([P, ne, DA, 8]),
-        )
-        nc.scalar.copy(
-            out=v_mat[:, :, :, 1:8],
-            in_=v_nat[:, 0:ne, :].unsqueeze(2).to_broadcast([P, ne, 16, DV]),
-        )
         gz_f = keep.tile([P, 4], F32)
-        nc.gpsimd.tensor_copy(out=gz_f[:], in_=gz_col[:])
-        nc.vector.tensor_copy(out=a_pad[:, 1:16, :], in_=a_nat[:].rearrange("p q c -> p c q"))
-        nc.gpsimd.tensor_copy(out=v_pad[:, 1:8, :], in_=v_nat[:].rearrange("p q c -> p c q"))
-        nc.gpsimd.tensor_copy(out=t_pad[:, 1:4, :], in_=t_nat[:].rearrange("p q c -> p c q"))
         sgn01 = keep.tile([P, 4], BF16)
         sgn = keep.tile([P, 4], BF16)
         gh_abs = keep.tile([P, 4], F32)
-        nc.gpsimd.tensor_scalar(out=sgn01[:], in0=gh_col[:], scalar1=0.0, scalar2=None, op0=ALU.is_ge)
-        nc.gpsimd.tensor_scalar(out=sgn[:], in0=sgn01[:], scalar1=2.0, scalar2=-1.0, op0=ALU.mult, op1=ALU.add)
-        nc.gpsimd.tensor_tensor(out=gh_abs[:], in0=gh_col[:], in1=sgn[:], op=ALU.mult)
-        for k in range(4):
-            nc.gpsimd.tensor_copy(
-                out=sel[32 * k : 32 * k + 1, k, :],
-                in_=gz_row[32 * k : 32 * k + 1, :].rearrange("o (p j) -> o j p", j=4)[:, k, :],
-            )
-
         tg = []
         for i in range(2):
             tgi = keep.tile([P, 4, CW], F32, name="tg%d" % i)
             tg.append(tgi)
+        nc.vector.memset(warm[:], 0.0)
+        nc.scalar.activation(out=warm2[:], in_=warm[:], func=ACT.Relu)
+
+        def ones_of(eng, c):
+            eng.memset(a_mats[c][:, :, 0, :], 1.0)
+            eng.memset(v_mats[c][:, :, :, 0], 1.0)
+
+        def mat_sources(c):
+            qs = slice(QC * c, QC * (c + 1))
+            return (
+                (v_mats[c][:, :, :, 1:8], v_nat[:, qs, :].unsqueeze(2).to_broadcast([P, QC, 16, DV])),
+                (a_mats[c][:, :, 1:16, :], a_nat[:, qs, :].unsqueeze(3).to_broadcast([P, QC, DA, 8])),
+            )
+
+        def g_copy(dst, src):
+            nc.gpsimd.tensor_scalar(out=dst, in0=src, scalar1=1.0, scalar2=0.0, op0=ALU.mult, op1=ALU.add)
+
+        ones_of(nc.vector, 0)
+        nc.vector.memset(a_pad[:, 0, :], 1.0)
+        nc.gpsimd.memset(ones[:], 1.0)
+        nc.gpsimd.memset(v_pad[:, 0, :], 1.0)
+        nc.gpsimd.memset(t_pad[:, 0, :], 1.0)
+        for c in range(1, EARLY):
+            ones_of(nc.gpsimd, c)
+        nc.vector.tensor_copy(out=gz_f[:], in_=gz_col[:])
+        for dst, src in mat_sources(0):
+            nc.vector.tensor_copy(out=dst, in_=src)
+        nc.vector.tensor_copy(out=a_pad[:, 1:16, :], in_=a_nat[:].rearrange("p q c -> p c q"))
+        g_copy(t_pad[:, 1:4, :], t_nat[:].rearrange("p q c -> p c q"))
+        for i in range(2):
+            nc.gpsimd.tensor_scalar(out=tg[i][:, 0, :], in0=ones[:], scalar1=gz_f[:, 0:1], scalar2=0.0, op0=ALU.mult, op1=ALU.add)
+        for c in (1, 2):
+            for dst, src in mat_sources(c):
+                g_copy(dst, src)
+        nc.gpsimd.tensor_scalar(out=sgn01[:], in0=gh_col[:], scalar1=0.0, scalar2=None, op0=ALU.is_ge)
+        nc.gpsimd.tensor_scalar(out=sgn[:], in0=sgn01[:], scalar1=2.0, scalar2=-1.0, op0=ALU.mult, op1=ALU.add)
+        nc.gpsimd.tensor_tensor(out=gh_abs[:], in0=gh_col[:], in1=sgn[:], op=ALU.mult)
+
         av_tiles = {}
         y_tiles = []
         zg_tiles = {}
@@ -112,24 +126,33 @@ def tile_tensorfusionouterproducthead_t_kernel(tc, a, v, t, gz, w1_bytes, w1_sca
         pieces = {}
         p1_tiles = {}
 
-        def early_factors(c):
-            a_ps = psum.tile([P, QC, P], BF16, name="a_ps", tag="p", bufs=3)
+        early_ps = {}
+
+        def early_turn(c):
+            a_ps = psum.tile([P, QC, P], BF16, name="a_ps", tag="p", bufs=PB)
             v_ps = psum.tile([P, QC, P], BF16, name="v_ps", tag="o", bufs=2)
             for j in range(QC):
-                nc.tensor.transpose(v_ps[:, j, :], v_mat[:, QC * c + j].rearrange("p i s -> p (i s)"), ident[:])
+                nc.tensor.transpose(v_ps[:, j, :], v_mats[c][:, j].rearrange("p i s -> p (i s)"), ident[:])
             for j in range(QC):
-                nc.tensor.transpose(a_ps[:, j, :], a_mat[:, QC * c + j].rearrange("p i s -> p (i s)"), ident[:])
+                nc.tensor.transpose(a_ps[:, j, :], a_mats[c][:, j].rearrange("p i s -> p (i s)"), ident[:])
             v_sb = work.tile([P, CW], BF16, name="v_sb", tag="v_sb", bufs=2)
-            nc.scalar.copy(out=v_sb[:], in_=v_ps[:].rearrange("p q h -> p (q h)"))
-            av = work.tile([P, CW], F32, name="av", tag="av", bufs=3)
+            if c == 0:
+                nc.vector.tensor_copy(out=v_sb[:], in_=v_ps[:].rearrange("p q h -> p (q h)"))
+            else:
+                nc.scalar.copy(out=v_sb[:], in_=v_ps[:].rearrange("p q h -> p (q h)"))
+            early_ps[c] = (a_ps, v_sb)
+
+        def early_mul(c):
+            a_ps, v_sb = early_ps[c]
+            av = work.tile([P, CW], F32, name="av", tag="av", bufs=AVB)
             nc.vector.tensor_tensor(out=av[:], in0=a_ps[:].rearrange("p q h -> p (q h)"), in1=v_sb[:], op=ALU.mult)
             av_tiles[c] = av
 
         def late_factors(c):
             ar, vr, r, base = pieces[c]
             lo = c * CW - base
-            av = work.tile([P, CW], F32, name="av", tag="av", bufs=3)
-            nc.vector.tensor_tensor(out=av[:], in0=ar[:, lo : lo + CW], in1=vr[:, lo : lo + CW], op=ALU.mult)
+            av = work.tile([P, CW], F32, name="av", tag="av", bufs=AVB)
+            nc.gpsimd.tensor_tensor(out=av[:], in0=ar[:, lo : lo + CW], in1=vr[:, lo : lo + CW], op=ALU.mult)
             av_tiles[c] = av
 
         def t_planes(c):
@@ -151,12 +174,12 @@ def tile_tensorfusionouterproducthead_t_kernel(tc, a, v, t, gz, w1_bytes, w1_sca
             for k in range(1, 4):
                 nc.tensor.matmul(y[:, k, :], lhsT=sel[:, k, :], rhs=r[:, lo : lo + P], start=True, stop=True)
 
-        def fuse(c, j):
+        def fuse(c, j, jn=1):
             if j == 0:
                 zg = work.tile([P, CW, 4], BF16, name="zg", tag="zg", bufs=2, align_bytes=64)
                 zg_tiles[c] = zg
-            cols = slice(j * P, (j + 1) * P)
-            x = av_tiles[c][:, cols].unsqueeze(2).to_broadcast([P, P, 4])
+            cols = slice(j * P, (j + jn) * P)
+            x = av_tiles[c][:, cols].unsqueeze(2).to_broadcast([P, jn * P, 4])
             if c < CTYPE:
                 y = tg[c % 2][:, :, cols]
             else:
@@ -176,7 +199,7 @@ def tile_tensorfusionouterproducthead_t_kernel(tc, a, v, t, gz, w1_bytes, w1_sca
                 hp_tiles[c] = hp
             hp = hp_tiles[c]
             for k in ks:
-                p1 = psum.tile([P, CW], F32, name="p1", tag="p", bufs=3)
+                p1 = psum.tile([P, CW], F32, name="p1", tag="p", bufs=PB)
                 nc.tensor.matmul_mx(
                     out=p1[:],
                     lhsT=w1_codes[:, k * P : (k + 1) * P].bitcast(FP8X4),
@@ -200,7 +223,9 @@ def tile_tensorfusionouterproducthead_t_kernel(tc, a, v, t, gz, w1_bytes, w1_sca
                 hi_tiles[c] = ht
             dst = hi_tiles[c][:, lo:hi, :].rearrange("p (c i) k -> p c k i", i=4)
             src = hp_tiles[c][:, :, lo:hi].rearrange("p k (c i) -> p c k i", i=4)
-            if eng == "v":
+            if eng == "g":
+                g_copy(dst, src)
+            elif eng == "v":
                 nc.vector.tensor_copy(out=dst, in_=src)
             else:
                 nc.scalar.copy(out=dst, in_=src)
@@ -242,40 +267,34 @@ def tile_tensorfusionouterproducthead_t_kernel(tc, a, v, t, gz, w1_bytes, w1_sca
             if store is not None:
                 nc.sync.dma_start(out=out_v[:, QC * c + store[0] : QC * c + store[1], :], in_=osb[:, store[0] : store[1], :])
 
-        early_factors(0)
         t_planes(0)
-        for i in range(2):
-            nc.vector.tensor_scalar(out=tg[i][:, 0, :], in0=ones[:], scalar1=gz_f[:, 0:1], scalar2=None, op0=ALU.mult)
-        turned = keep.tile([P, 14, P], BF16)
-        src_cols = [a_pad[:].rearrange("p c q -> p (c q)"), v_pad[:].rearrange("p c q -> p (c q)"), t_pad[:].rearrange("p c q -> p (c q)")]
-        m = 0
-        for cols_ap, cnt in ((src_cols[0], 4), (src_cols[0], 4), (src_cols[1], 4), (src_cols[2], 2)):
-            first = 4 if m == 4 else 0
-            tp = psum.tile([P, 4, P], BF16, name="tp", tag="p", bufs=3)
-            for i in range(cnt):
-                nc.tensor.transpose(tp[:, i, :], cols_ap[:, (first + i) * P : (first + i + 1) * P], ident[:])
-            nc.scalar.copy(out=turned[:, m : m + cnt, :], in_=tp[:, 0:cnt, :])
-            m += cnt
-        park_rows = 14 * P * P // 2 // O
-        park = out[N - park_rows : N, :].rearrange("r o -> (r o)").bitcast(BF16)
-        nc.sync.dma_start(out=park.rearrange("(m p h) -> p m h", p=P, h=P), in_=turned[:])
-        a_park = park[0 : 16 * N].rearrange("(i n) -> i n", i=16)
-        for c0, c1 in ((2, 4), (4, 8), (8, 16)):
-            n0, n1 = c0 * CW, c1 * CW
-            w = n1 - n0
-            ar = keep.tile([P, w], BF16, name="ar%d" % c0)
-            vr = keep.tile([P, w], BF16, name="vr%d" % c0)
-            r = None
-            for s in range(8):
-                nc.sync.dma_start(out=ar[s:P:8, :], in_=a_park[:, n0:n1])
-            for s in range(8):
-                nc.sync.dma_start(out=vr[s:P:8, :], in_=park[(16 + s) * N + n0 : (16 + s) * N + n1].partition_broadcast(16))
-            if c0 >= CTYPE:
+        early_turn(0)
+        early_mul(0)
+        def bounce():
+            turned = keep.tile([P, 14, P], BF16)
+            src_cols = [a_pad[:].rearrange("p c q -> p (c q)"), v_pad[:].rearrange("p c q -> p (c q)"), t_pad[:].rearrange("p c q -> p (c q)")]
+            m = 0
+            for cols_ap, cnt in ((src_cols[0], 4), (src_cols[0], 4), (src_cols[1], 4), (src_cols[2], 2)):
+                first = 4 if m == 4 else 0
+                tp = psum.tile([P, 4, P], BF16, name="tp", tag="p", bufs=PB)
+                for i in range(cnt):
+                    nc.tensor.transpose(tp[:, i, :], cols_ap[:, (first + i) * P : (first + i + 1) * P], ident[:])
+                nc.scalar.copy(out=turned[:, m : m + cnt, :], in_=tp[:, 0:cnt, :])
+                m += cnt
+            park_rows = 14 * P * P // 2 // O
+            park = out[N - park_rows : N, :].rearrange("r o -> (r o)").bitcast(BF16)
+            nc.sync.dma_start(out=park.rearrange("(m p h) -> p m h", p=P, h=P), in_=turned[:])
+            for c0, c1 in ((4, 8), (8, 16)):
+                n0, n1 = c0 * CW, c1 * CW
+                w = n1 - n0
+                ar = keep.tile([P, w], BF16, name="ar%d" % c0)
+                vr = keep.tile([P, w], BF16, name="vr%d" % c0)
                 r = keep.tile([P, w], BF16, name="r%d" % c0)
-                for k in range(4):
-                    nc.sync.dma_start(out=r[32 * k : 32 * k + 32, :], in_=park[(24 + k) * N + n0 : (24 + k) * N + n1].partition_broadcast(32))
-            for c in range(c0, c1):
-                pieces[c] = (ar, vr, r, n0)
+                nc.sync.dma_start(out=r[:], in_=park[24 * N : 28 * N].rearrange("(k n) -> k n", k=4)[:, n0:n1].unsqueeze(1).to_broadcast([4, 32, w]))
+                nc.sync.dma_start(out=ar[:], in_=park[0 : 16 * N].rearrange("(i n) -> i n", i=16)[:, n0:n1].unsqueeze(1).to_broadcast([16, 8, w]))
+                nc.sync.dma_start(out=vr[:], in_=park[16 * N : 24 * N].rearrange("(j n) -> j n", j=8)[:, n0:n1].unsqueeze(0).to_broadcast([16, 8, w]))
+                for c in range(c0, c1):
+                    pieces[c] = (ar, vr, r, n0)
 
         w1_wide = keep.tile([P, 4, H], BF16)
         w1_grp = keep.tile([P, H, 4], BF16, align_bytes=64)
@@ -284,43 +303,61 @@ def tile_tensorfusionouterproducthead_t_kernel(tc, a, v, t, gz, w1_bytes, w1_sca
         w2_grp = keep.tile([P, O, 4], BF16, align_bytes=64)
         w2_codes = keep.tile([P, O], U32, align_bytes=64)
         w2_scales = keep.tile([P, O], U8, align_bytes=64)
-        for k in range(4):
-            nc.scalar.activation(out=w1_wide[:, k, :], in_=w1_raw[:, k, :].bitcast(FP8), func=ACT.Copy, scale=w1_sc[:, k : k + 1])
 
-        def weights1():
-            nc.vector.tensor_copy(
-                out=w1_grp[:].rearrange("p (k m) j -> p k m j", k=4),
-                in_=w1_wide[:].rearrange("p j (m k) -> p k m j", k=4),
-            )
+        def weights_s(ks):
+            for k in ks:
+                nc.scalar.activation(out=w1_wide[:, k, :], in_=w1_raw[:, k, :].bitcast(FP8), func=ACT.Copy, scale=w1_sc[:, k : k + 1])
 
-        def weights2():
-            nc.vector.tensor_tensor(
+        def weights_g():
+            nc.gpsimd.tensor_tensor(
                 out=w2_grp[:],
                 in0=w2_raw[:].rearrange("p j n -> p n j"),
                 in1=sgn[:].unsqueeze(1).to_broadcast([P, O, 4]),
                 op=ALU.mult,
             )
-            nc.vector.quantize_mx(out=w1_codes[:].bitcast(FP8X4), scales=w1_scales[:], in_=w1_grp[:].rearrange("p n j -> p (n j)"))
+            g_copy(v_pad[:, 1:8, :], v_nat[:].rearrange("p q c -> p c q"))
+            g_copy(w1_grp[:].rearrange("p (k m) j -> p k m j", k=4), w1_wide[:].rearrange("p j (m k) -> p k m j", k=4))
+            for dst, src in mat_sources(3):
+                g_copy(dst, src)
+            nc.gpsimd.memset(sel[:], 0.0)
+            for k in range(4):
+                nc.gpsimd.tensor_copy(
+                    out=sel[32 * k : 32 * k + 1, k, :],
+                    in_=gz_row[32 * k : 32 * k + 1, :].rearrange("o (p j) -> o j p", j=4)[:, k, :],
+                )
 
-        def weights3():
+        def weights_q():
             nc.vector.quantize_mx(out=w2_codes[:].bitcast(FP8X4), scales=w2_scales[:], in_=w2_grp[:].rearrange("p n j -> p (n j)"))
+            nc.vector.quantize_mx(out=w1_codes[:].bitcast(FP8X4), scales=w1_scales[:], in_=w1_grp[:].rearrange("p n j -> p (n j)"))
 
         for r in range(NCH):
             if r >= 1:
                 fuse(r - 1, 3)
             if CTYPE <= r:
                 y_block(r, 2)
-            for j in range(3):
-                fuse(r, j)
+            if r < CTYPE:
+                fuse(r, 0, 3)
+            else:
+                for j in range(3):
+                    fuse(r, j)
             if r == 0:
-                weights1()
-            if r + 1 < NCH:
-                if r + 1 < EARLY:
-                    early_factors(r + 1)
-                else:
-                    late_factors(r + 1)
+                weights_s((0, 1, 2))
+                early_turn(1)
+                early_mul(1)
+                t_planes(1)
+                weights_s((3,))
+                weights_g()
+                early_turn(2)
+                bounce()
+            elif r + 1 < NCH:
+                if r + 1 < EARLY and r + 1 != 3:
+                    early_mul(r + 1)
+                if r == 2:
+                    early_turn(3)
                 if r + 1 < CTYPE:
                     t_planes(r + 1)
+                else:
+                    late_factors(r + 1)
             if r == CTYPE - 1:
                 for i in range(3):
                     y = psum.tile([P, 4, P], F32, name="y%d" % i, tag="y%d" % i, bufs=1)
@@ -331,9 +368,9 @@ def tile_tensorfusionouterproducthead_t_kernel(tc, a, v, t, gz, w1_bytes, w1_sca
             if CTYPE <= r + 1 < NCH:
                 y_block(r + 1, 0)
                 y_block(r + 1, 1)
-            if r == 0:
-                weights2()
             if 0 <= r - 2 < NCH - 2:
+                if ILG:
+                    interleave("g", r - 2, 0, ILG)
                 interleave("s", r - 2, ILV, CW)
             if 0 <= r - 3 < NCH - 3:
                 quant_h(r - 3)
@@ -341,26 +378,29 @@ def tile_tensorfusionouterproducthead_t_kernel(tc, a, v, t, gz, w1_bytes, w1_sca
                 stage2(r - 3, 1, store=(0, 4))
             if 0 <= r - 1 < NCH - 1:
                 quant_z(r - 1)
+                if r == 1:
+                    weights_q()
                 stage1(r - 1, range(4))
-            if r == 0:
-                weights3()
             if 0 <= r - 2 < NCH - 2:
-                interleave("v", r - 2, 0, ILV)
+                interleave("v", r - 2, ILG, ILV)
+            if r == 2:
+                early_mul(3)
         last = NCH - 1
         fuse(last, 3)
-        quant_z(last)
-        stage1(last, (0, 1, 2), (2,))
         quant_h(last - 2)
+        quant_z(last)
+        interleave("s", last - 1, 384, CW)
+        stage1(last, (0, 1, 2), (2,))
         stage2(last - 2, 0)
         stage2(last - 2, 1, store=(0, 4))
         stage1(last, (3,), (3,))
-        interleave("v", last - 1, 0, CW)
+        interleave("v", last - 1, 0, 384)
         relu_v(last, 2)
         relu_v(last, 3)
         quant_h(last - 1)
         stage2(last - 1, 0)
-        interleave("v", last, 0, CW // 2)
         stage2(last - 1, 1, store=(0, 4))
+        interleave("v", last, 0, CW // 2)
         interleave("v", last, CW // 2, CW)
         quant_h(last, 0, CW // 2)
         stage2(last, 0, store=(0, 2))

@@ -18,12 +18,19 @@ QS = N // P
 NCH = 16
 QC = QS // NCH
 CW = QC * P
-EARLY = 4
+EARLY = 3
 CTYPE = 4
-ILG = 192
-ILV = 400
+ILG = 0
+ILV = 384
 AVB = 2
-PB = 3
+GAV = 5
+PB = 2
+YB = 4
+QB = 2
+CB = 2
+HB = 3
+LQ = 4
+LI = 3
 FLOPS = 2 * N * Z * H + 2 * N * H * O
 
 
@@ -81,6 +88,10 @@ def tile_tensorfusionouterproducthead_t_kernel(tc, a, v, t, gz, w1_bytes, w1_sca
         nc.vector.memset(warm[:], 0.0)
         nc.scalar.activation(out=warm2[:], in_=warm[:], func=ACT.Relu)
 
+        MATS = (nc.vector, nc.scalar, nc.scalar)
+        PADS = nc.vector
+        PADT = nc.vector
+
         def ones_of(eng, c):
             eng.memset(a_mats[c][:, :, 0, :], 1.0)
             eng.memset(v_mats[c][:, :, :, 0], 1.0)
@@ -95,34 +106,47 @@ def tile_tensorfusionouterproducthead_t_kernel(tc, a, v, t, gz, w1_bytes, w1_sca
         def g_copy(dst, src):
             nc.gpsimd.tensor_scalar(out=dst, in0=src, scalar1=1.0, scalar2=0.0, op0=ALU.mult, op1=ALU.add)
 
-        ones_of(nc.vector, 0)
-        nc.vector.memset(a_pad[:, 0, :], 1.0)
+        for c in range(EARLY):
+            ones_of(nc.vector, c)
+        PADS.memset(a_pad[:, 0, :], 1.0)
         nc.gpsimd.memset(ones[:], 1.0)
         nc.gpsimd.memset(v_pad[:, 0, :], 1.0)
         nc.gpsimd.memset(t_pad[:, 0, :], 1.0)
-        for c in range(1, EARLY):
-            ones_of(nc.gpsimd, c)
+        nc.gpsimd.memset(sel[:], 0.0)
         nc.vector.tensor_copy(out=gz_f[:], in_=gz_col[:])
-        for dst, src in mat_sources(0):
-            nc.vector.tensor_copy(out=dst, in_=src)
-        nc.vector.tensor_copy(out=a_pad[:, 1:16, :], in_=a_nat[:].rearrange("p q c -> p c q"))
-        g_copy(t_pad[:, 1:4, :], t_nat[:].rearrange("p q c -> p c q"))
-        for i in range(2):
-            nc.gpsimd.tensor_scalar(out=tg[i][:, 0, :], in0=ones[:], scalar1=gz_f[:, 0:1], scalar2=0.0, op0=ALU.mult, op1=ALU.add)
-        for c in (1, 2):
+
+        def put(eng, dst, src):
+            if eng is nc.vector:
+                nc.vector.tensor_copy(out=dst, in_=src)
+            else:
+                nc.scalar.copy(out=dst, in_=src)
+
+        def mat(c):
             for dst, src in mat_sources(c):
-                g_copy(dst, src)
-        nc.gpsimd.tensor_scalar(out=sgn01[:], in0=gh_col[:], scalar1=0.0, scalar2=None, op0=ALU.is_ge)
-        nc.gpsimd.tensor_scalar(out=sgn[:], in0=sgn01[:], scalar1=2.0, scalar2=-1.0, op0=ALU.mult, op1=ALU.add)
-        nc.gpsimd.tensor_tensor(out=gh_abs[:], in0=gh_col[:], in1=sgn[:], op=ALU.mult)
+                put(MATS[c], dst, src)
+
+        def consts(i):
+            nc.vector.tensor_scalar(out=tg[i][:, 0, :], in0=ones[:], scalar1=gz_f[:, 0:1], scalar2=None, op0=ALU.mult)
+
+        def pads():
+            put(PADT, t_pad[:, 1:4, :], t_nat[:].rearrange("p q c -> p c q"))
+            put(PADT, v_pad[:, 1:8, :], v_nat[:].rearrange("p q c -> p c q"))
+            put(PADS, a_pad[:, 1:16, :], a_nat[:].rearrange("p q c -> p c q"))
+
+        def small():
+            nc.gpsimd.tensor_scalar(out=sgn01[:], in0=gh_col[:], scalar1=0.0, scalar2=None, op0=ALU.is_ge)
+            nc.gpsimd.tensor_scalar(out=sgn[:], in0=sgn01[:], scalar1=2.0, scalar2=-1.0, op0=ALU.mult, op1=ALU.add)
+            nc.gpsimd.tensor_tensor(out=gh_abs[:], in0=gh_col[:], in1=sgn[:], op=ALU.mult)
+            for k in range(4):
+                nc.gpsimd.tensor_scalar(
+                    out=sel[32 * k : 32 * k + 1, k, :],
+                    in0=gz_row[32 * k : 32 * k + 1, :].rearrange("o (p j) -> o j p", j=4)[:, k, :],
+                    scalar1=1.0, scalar2=0.0, op0=ALU.mult, op1=ALU.add,
+                )
 
         av_tiles = {}
         y_tiles = []
-        zg_tiles = {}
-        zc_tiles = {}
         hp_tiles = {}
-        hi_tiles = {}
-        hc_tiles = {}
         pieces = {}
         p1_tiles = {}
 
@@ -152,7 +176,7 @@ def tile_tensorfusionouterproducthead_t_kernel(tc, a, v, t, gz, w1_bytes, w1_sca
             ar, vr, r, base = pieces[c]
             lo = c * CW - base
             av = work.tile([P, CW], F32, name="av", tag="av", bufs=AVB)
-            nc.gpsimd.tensor_tensor(out=av[:], in0=ar[:, lo : lo + CW], in1=vr[:, lo : lo + CW], op=ALU.mult)
+            (nc.vector if c < GAV else nc.gpsimd).tensor_tensor(out=av[:], in0=ar[:, lo : lo + CW], in1=vr[:, lo : lo + CW], op=ALU.mult)
             av_tiles[c] = av
 
         def t_planes(c):
@@ -170,32 +194,41 @@ def tile_tensorfusionouterproducthead_t_kernel(tc, a, v, t, gz, w1_bytes, w1_sca
         def y_block(c, j):
             ar, vr, r, base = pieces[c]
             lo = c * CW - base + j * P
-            y = y_tiles[(QC * c + j) % 3]
+            y = y_tiles[(QC * c + j) % YB]
             for k in range(1, 4):
                 nc.tensor.matmul(y[:, k, :], lhsT=sel[:, k, :], rhs=r[:, lo : lo + P], start=True, stop=True)
 
         def fuse(c, j, jn=1):
-            if j == 0:
-                zg = work.tile([P, CW, 4], BF16, name="zg", tag="zg", bufs=2, align_bytes=64)
-                zg_tiles[c] = zg
+            zg = qin(c + 1)[:, 0:CW, :]
             cols = slice(j * P, (j + jn) * P)
             x = av_tiles[c][:, cols].unsqueeze(2).to_broadcast([P, jn * P, 4])
             if c < CTYPE:
                 y = tg[c % 2][:, :, cols]
             else:
-                y = y_tiles[(QC * c + j) % 3][:]
-            nc.vector.tensor_tensor(out=zg_tiles[c][:, cols, :], in0=y.rearrange("p k n -> p n k"), in1=x, op=ALU.mult)
+                y = y_tiles[(QC * c + j) % YB][:]
+            nc.vector.tensor_tensor(out=zg[:, cols, :], in0=y.rearrange("p k n -> p n k"), in1=x, op=ALU.mult)
 
-        def quant_z(c):
-            zc = work.tile([P, CW], U32, name="zc", tag="zc", bufs=2, align_bytes=64)
-            zs = work.tile([P, CW], U8, name="zs", tag="zs", bufs=2, align_bytes=64)
-            nc.vector.quantize_mx(out=zc[:].bitcast(FP8X4), scales=zs[:], in_=zg_tiles[c][:].rearrange("p n k -> p (n k)"))
-            zc_tiles[c] = (zc, zs)
+        q_tiles = {}
+        c_tiles = {}
+
+        def qin(r):
+            if r not in q_tiles:
+                qt = work.tile([P, 2 * CW, 4], BF16, name="qt", tag="qt", bufs=QB, align_bytes=64)
+                q_tiles[r] = qt
+            return q_tiles[r]
+
+        def quant(r, lo, hi):
+            if r not in c_tiles:
+                qc = work.tile([P, 2 * CW], U32, name="qc", tag="qc", bufs=CB, align_bytes=64)
+                qs = work.tile([P, 2 * CW], U8, name="qs", tag="qs", bufs=CB, align_bytes=64)
+                c_tiles[r] = (qc, qs)
+            qc, qs = c_tiles[r]
+            nc.vector.quantize_mx(out=qc[:, lo:hi].bitcast(FP8X4), scales=qs[:, lo:hi], in_=qin(r)[:, lo:hi, :].rearrange("p n k -> p (n k)"))
 
         def stage1(c, ks, vec_ks=()):
-            zc, zs = zc_tiles[c]
+            zc, zs = c_tiles[c + 1]
             if c not in hp_tiles:
-                hp = work.tile([P, 4, CW], BF16, name="hp", tag="hp", bufs=2)
+                hp = work.tile([P, 4, CW], BF16, name="hp", tag="hp", bufs=HB)
                 hp_tiles[c] = hp
             hp = hp_tiles[c]
             for k in ks:
@@ -204,8 +237,8 @@ def tile_tensorfusionouterproducthead_t_kernel(tc, a, v, t, gz, w1_bytes, w1_sca
                     out=p1[:],
                     lhsT=w1_codes[:, k * P : (k + 1) * P].bitcast(FP8X4),
                     lhsT_scale=w1_scales[:, k * P : (k + 1) * P],
-                    rhs=zc[:].bitcast(FP8X4),
-                    rhs_scale=zs[:],
+                    rhs=zc[:, 0:CW].bitcast(FP8X4),
+                    rhs_scale=zs[:, 0:CW],
                     start=True,
                     stop=True,
                 )
@@ -218,10 +251,7 @@ def tile_tensorfusionouterproducthead_t_kernel(tc, a, v, t, gz, w1_bytes, w1_sca
                                     op0=ALU.max, op1=ALU.mult)
 
         def interleave(eng, c, lo, hi):
-            if c not in hi_tiles:
-                ht = work.tile([P, CW, 4], BF16, name="ht", tag="ht", bufs=2, align_bytes=64)
-                hi_tiles[c] = ht
-            dst = hi_tiles[c][:, lo:hi, :].rearrange("p (c i) k -> p c k i", i=4)
+            dst = qin(c + LQ)[:, CW + lo : CW + hi, :].rearrange("p (c i) k -> p c k i", i=4)
             src = hp_tiles[c][:, :, lo:hi].rearrange("p k (c i) -> p c k i", i=4)
             if eng == "g":
                 g_copy(dst, src)
@@ -230,27 +260,18 @@ def tile_tensorfusionouterproducthead_t_kernel(tc, a, v, t, gz, w1_bytes, w1_sca
             else:
                 nc.scalar.copy(out=dst, in_=src)
 
-        def quant_h(c, lo=0, hi=CW):
-            if c not in hc_tiles:
-                hc = work.tile([P, CW], U32, name="hc", tag="hc", bufs=2, align_bytes=64)
-                hs = work.tile([P, CW], U8, name="hs", tag="hs", bufs=2, align_bytes=64)
-                hc_tiles[c] = (hc, hs)
-            hc, hs = hc_tiles[c]
-            nc.vector.quantize_mx(out=hc[:, lo:hi].bitcast(FP8X4), scales=hs[:, lo:hi],
-                                  in_=hi_tiles[c][:, lo:hi, :].rearrange("p n k -> p (n k)"))
-
         out_v = out.rearrange("(h q) o -> h q o", q=QS)
         o_tiles = {}
 
         def stage2(c, jj, vec=False, store=None):
-            hc, hs = hc_tiles[c]
+            hc, hs = c_tiles[c + LQ]
             if c not in o_tiles:
-                osb = work.tile([P, QC, O], F32, name="osb", tag="osb", bufs=3)
+                osb = work.tile([P, QC, O], F32, name="osb", tag="osb", bufs=4)
                 o_tiles[c] = osb
             osb = o_tiles[c]
             po = psum.tile([P, 2, O], F32, name="po", tag="o", bufs=2)
             for j in range(2):
-                cols = slice((2 * jj + j) * P, (2 * jj + j + 1) * P)
+                cols = slice(CW + (2 * jj + j) * P, CW + (2 * jj + j + 1) * P)
                 nc.tensor.matmul_mx(
                     out=po[:, j, :],
                     lhsT=hc[:, cols].bitcast(FP8X4),
@@ -267,6 +288,8 @@ def tile_tensorfusionouterproducthead_t_kernel(tc, a, v, t, gz, w1_bytes, w1_sca
             if store is not None:
                 nc.sync.dma_start(out=out_v[:, QC * c + store[0] : QC * c + store[1], :], in_=osb[:, store[0] : store[1], :])
 
+        mat(0)
+        consts(0)
         t_planes(0)
         early_turn(0)
         early_mul(0)
@@ -284,13 +307,14 @@ def tile_tensorfusionouterproducthead_t_kernel(tc, a, v, t, gz, w1_bytes, w1_sca
             park_rows = 14 * P * P // 2 // O
             park = out[N - park_rows : N, :].rearrange("r o -> (r o)").bitcast(BF16)
             nc.sync.dma_start(out=park.rearrange("(m p h) -> p m h", p=P, h=P), in_=turned[:])
-            for c0, c1 in ((4, 8), (8, 16)):
+            for c0, c1 in ((3, 4), (4, 8), (8, 16)):
                 n0, n1 = c0 * CW, c1 * CW
                 w = n1 - n0
                 ar = keep.tile([P, w], BF16, name="ar%d" % c0)
                 vr = keep.tile([P, w], BF16, name="vr%d" % c0)
                 r = keep.tile([P, w], BF16, name="r%d" % c0)
-                nc.sync.dma_start(out=r[:], in_=park[24 * N : 28 * N].rearrange("(k n) -> k n", k=4)[:, n0:n1].unsqueeze(1).to_broadcast([4, 32, w]))
+                if c0 >= CTYPE:
+                    nc.sync.dma_start(out=r[:], in_=park[24 * N : 28 * N].rearrange("(k n) -> k n", k=4)[:, n0:n1].unsqueeze(1).to_broadcast([4, 32, w]))
                 nc.sync.dma_start(out=ar[:], in_=park[0 : 16 * N].rearrange("(i n) -> i n", i=16)[:, n0:n1].unsqueeze(1).to_broadcast([16, 8, w]))
                 nc.sync.dma_start(out=vr[:], in_=park[16 * N : 24 * N].rearrange("(j n) -> j n", j=8)[:, n0:n1].unsqueeze(0).to_broadcast([16, 8, w]))
                 for c in range(c0, c1):
@@ -308,23 +332,16 @@ def tile_tensorfusionouterproducthead_t_kernel(tc, a, v, t, gz, w1_bytes, w1_sca
             for k in ks:
                 nc.scalar.activation(out=w1_wide[:, k, :], in_=w1_raw[:, k, :].bitcast(FP8), func=ACT.Copy, scale=w1_sc[:, k : k + 1])
 
-        def weights_g():
-            nc.gpsimd.tensor_tensor(
+        def weights_w2():
+            nc.vector.tensor_tensor(
                 out=w2_grp[:],
                 in0=w2_raw[:].rearrange("p j n -> p n j"),
                 in1=sgn[:].unsqueeze(1).to_broadcast([P, O, 4]),
                 op=ALU.mult,
             )
-            g_copy(v_pad[:, 1:8, :], v_nat[:].rearrange("p q c -> p c q"))
-            g_copy(w1_grp[:].rearrange("p (k m) j -> p k m j", k=4), w1_wide[:].rearrange("p j (m k) -> p k m j", k=4))
-            for dst, src in mat_sources(3):
-                g_copy(dst, src)
-            nc.gpsimd.memset(sel[:], 0.0)
-            for k in range(4):
-                nc.gpsimd.tensor_copy(
-                    out=sel[32 * k : 32 * k + 1, k, :],
-                    in_=gz_row[32 * k : 32 * k + 1, :].rearrange("o (p j) -> o j p", j=4)[:, k, :],
-                )
+
+        def weights_w1():
+            nc.vector.tensor_copy(out=w1_grp[:].rearrange("p (k m) j -> p k m j", k=4), in_=w1_wide[:].rearrange("p j (m k) -> p k m j", k=4))
 
         def weights_q():
             nc.vector.quantize_mx(out=w2_codes[:].bitcast(FP8X4), scales=w2_scales[:], in_=w2_grp[:].rearrange("p n j -> p (n j)"))
@@ -333,76 +350,75 @@ def tile_tensorfusionouterproducthead_t_kernel(tc, a, v, t, gz, w1_bytes, w1_sca
         for r in range(NCH):
             if r >= 1:
                 fuse(r - 1, 3)
-            if CTYPE <= r:
-                y_block(r, 2)
             if r < CTYPE:
                 fuse(r, 0, 3)
             else:
                 for j in range(3):
                     fuse(r, j)
             if r == 0:
-                weights_s((0, 1, 2))
+                mat(1)
                 early_turn(1)
                 early_mul(1)
+                consts(1)
                 t_planes(1)
-                weights_s((3,))
-                weights_g()
-                early_turn(2)
+                pads()
+                small()
+                weights_s((0, 1, 2, 3))
+                weights_w2()
                 bounce()
-            elif r + 1 < NCH:
-                if r + 1 < EARLY and r + 1 != 3:
-                    early_mul(r + 1)
-                if r == 2:
-                    early_turn(3)
+                mat(2)
+                early_turn(2)
+            else:
+                if EARLY <= r + 1 < NCH:
+                    late_factors(r + 1)
                 if r + 1 < CTYPE:
                     t_planes(r + 1)
-                else:
-                    late_factors(r + 1)
+            if r == 1:
+                weights_w1()
             if r == CTYPE - 1:
-                for i in range(3):
+                for i in range(YB):
                     y = psum.tile([P, 4, P], F32, name="y%d" % i, tag="y%d" % i, bufs=1)
                     nc.tensor.matmul(y[:, 0, :], lhsT=sel[:, 0, :], rhs=pieces[CTYPE][2][:, 0:P], start=True, stop=True)
                     y_tiles.append(y)
             if CTYPE <= r:
                 y_block(r, 3)
             if CTYPE <= r + 1 < NCH:
-                y_block(r + 1, 0)
-                y_block(r + 1, 1)
-            if 0 <= r - 2 < NCH - 2:
-                if ILG:
-                    interleave("g", r - 2, 0, ILG)
-                interleave("s", r - 2, ILV, CW)
-            if 0 <= r - 3 < NCH - 3:
-                quant_h(r - 3)
-                stage2(r - 3, 0)
-                stage2(r - 3, 1, store=(0, 4))
-            if 0 <= r - 1 < NCH - 1:
-                quant_z(r - 1)
+                for j in range(3):
+                    y_block(r + 1, j)
+            if 0 <= r - LI < NCH - 3:
+                interleave("s", r - LI, ILV, CW)
+            if r >= 1:
+                quant(r, 0, 2 * CW if r >= LQ else CW)
                 if r == 1:
                     weights_q()
                 stage1(r - 1, range(4))
-            if 0 <= r - 2 < NCH - 2:
-                interleave("v", r - 2, ILG, ILV)
-            if r == 2:
-                early_mul(3)
+            if 0 <= r - LQ:
+                stage2(r - LQ, 0)
+                stage2(r - LQ, 1, store=(0, 4))
+            if 0 <= r - LI < NCH - 3:
+                interleave("v", r - LI, ILG, ILV)
+            if r == 1:
+                early_mul(2)
         last = NCH - 1
         fuse(last, 3)
-        quant_h(last - 2)
-        quant_z(last)
-        interleave("s", last - 1, 384, CW)
+        quant(NCH, 0, 2 * CW)
         stage1(last, (0, 1, 2), (2,))
-        stage2(last - 2, 0)
-        stage2(last - 2, 1, store=(0, 4))
+        stage2(last - 3, 0)
+        stage2(last - 3, 1, store=(0, 4))
         stage1(last, (3,), (3,))
-        interleave("v", last - 1, 0, 384)
+        interleave("v", last - 2, 0, 512)
+        interleave("v", last - 1, 0, 512)
+        quant(NCH + 1, CW, 2 * CW)
+        stage2(last - 2, 0)
         relu_v(last, 2)
         relu_v(last, 3)
-        quant_h(last - 1)
+        quant(NCH + 2, CW, 2 * CW)
+        stage2(last - 2, 1, store=(0, 4))
         stage2(last - 1, 0)
         stage2(last - 1, 1, store=(0, 4))
-        interleave("v", last, 0, CW // 2)
-        interleave("v", last, CW // 2, CW)
-        quant_h(last, 0, CW // 2)
+        interleave("v", last, 0, 256)
+        interleave("v", last, 256, 512)
+        quant(NCH + 3, CW, CW + 256)
         stage2(last, 0, store=(0, 2))
-        quant_h(last, CW // 2, CW)
+        quant(NCH + 3, CW + 256, 2 * CW)
         stage2(last, 1, vec=True, store=(2, 4))

from contextlib import ExitStack

import concourse.mybir as mybir
from concourse.masks import make_identity

F32 = mybir.dt.float32
BF16 = mybir.dt.bfloat16
U32 = mybir.dt.uint32
U8 = mybir.dt.uint8
FP8 = mybir.dt.float8_e4m3fn
FP8X4 = mybir.dt.float8_e4m3fn_x4
ALU = mybir.AluOpType
ACT = mybir.ActivationFunctionType

N, DA, DV, DT, Z, H, O = 8192, 15, 7, 3, 512, 512, 256
P = 128
QS = N // P
NCH = 16
QC = QS // NCH
CW = QC * P
EARLY = 3
CTYPE = 4
ILG = 0
ILV = 384
AVB = 2
GAV = 5
PB = 2
YB = 4
QB = 2
CB = 2
HB = 3
LQ = 4
LI = 3
FLOPS = 2 * N * Z * H + 2 * N * H * O


def tile_tensorfusionouterproducthead_t_kernel(tc, a, v, t, gz, w1_bytes, w1_scale, gh, w2, out):
    nc = tc.nc
    with ExitStack() as ctx:
        keep = ctx.enter_context(tc.tile_pool(name="keep", bufs=1))
        work = ctx.enter_context(tc.tile_pool(name="work", bufs=2))
        psum = ctx.enter_context(tc.psum_pool(name="psum", bufs=1))
        ctx.enter_context(tc.manual_schedule())

        t_nat = keep.tile([P, QS, DT], BF16)
        v_nat = keep.tile([P, QS, DV], BF16)
        a_nat = keep.tile([P, QS, DA], BF16)
        gz_col = keep.tile([P, 4], BF16)
        gz_row = keep.tile([P, Z], BF16)
        gh_col = keep.tile([P, 4], BF16)
        w1_raw = keep.tile([P, 4, H], U8)
        w1_sc = keep.tile([P, 4], F32)
        w2_raw = keep.tile([P, 4, O], BF16)
        nc.sync.dma_start(out=t_nat[:], in_=t.rearrange("(h q) c -> h q c", q=QS))
        nc.sync.dma_start(out=gz_col[:], in_=gz.rearrange("(p j) -> p j", j=4))
        nc.sync.dma_start(out=v_nat[:], in_=v.rearrange("(h q) c -> h q c", q=QS))
        nc.sync.dma_start(out=a_nat[:], in_=a.rearrange("(h q) c -> h q c", q=QS))
        nc.sync.dma_start(out=w1_sc[:], in_=w1_scale.rearrange("(p j) o -> p (j o)", j=4))
        nc.sync.dma_start(out=w1_raw[:], in_=w1_bytes.rearrange("(p j) n -> p j n", j=4))
        nc.sync.dma_start(out=gh_col[:], in_=gh.rearrange("(p j) -> p j", j=4))
        nc.sync.dma_start(out=w2_raw[:], in_=w2.rearrange("(p j) n -> p j n", j=4))
        nc.sync.dma_start(out=gz_row[:], in_=gz.partition_broadcast(P))

        ident = keep.tile([P, P], BF16)
        make_identity(nc, ident[:])
        a_mats = []
        v_mats = []
        for c in range(EARLY):
            am = keep.tile([P, QC, 16, 8], BF16, name="a_mat%d" % c)
            vm = keep.tile([P, QC, 16, 8], BF16, name="v_mat%d" % c)
            a_mats.append(am)
            v_mats.append(vm)
        a_pad = keep.tile([P, 16, QS], BF16)
        v_pad = keep.tile([P, 8, QS], BF16)
        t_pad = keep.tile([P, 4, QS], BF16)
        sel = keep.tile([P, 4, P], BF16)
        ones = keep.tile([P, CW], BF16)
        warm = keep.tile([P, 1], F32)
        warm2 = keep.tile([P, 1], F32)
        gz_f = keep.tile([P, 4], F32)
        sgn01 = keep.tile([P, 4], BF16)
        sgn = keep.tile([P, 4], BF16)
        gh_abs = keep.tile([P, 4], F32)
        tg = []
        for i in range(2):
            tgi = keep.tile([P, 4, CW], F32, name="tg%d" % i)
            tg.append(tgi)
        nc.vector.memset(warm[:], 0.0)
        nc.scalar.activation(out=warm2[:], in_=warm[:], func=ACT.Relu)

        MATS = (nc.vector, nc.scalar, nc.scalar)
        PADS = nc.vector
        PADT = nc.vector

        def ones_of(eng, c):
            eng.memset(a_mats[c][:, :, 0, :], 1.0)
            eng.memset(v_mats[c][:, :, :, 0], 1.0)

        def mat_sources(c):
            qs = slice(QC * c, QC * (c + 1))
            return (
                (v_mats[c][:, :, :, 1:8], v_nat[:, qs, :].unsqueeze(2).to_broadcast([P, QC, 16, DV])),
                (a_mats[c][:, :, 1:16, :], a_nat[:, qs, :].unsqueeze(3).to_broadcast([P, QC, DA, 8])),
            )

        def g_copy(dst, src):
            nc.gpsimd.tensor_scalar(out=dst, in0=src, scalar1=1.0, scalar2=0.0, op0=ALU.mult, op1=ALU.add)

        for c in range(EARLY):
            ones_of(nc.vector, c)
        PADS.memset(a_pad[:, 0, :], 1.0)
        nc.gpsimd.memset(ones[:], 1.0)
        nc.gpsimd.memset(v_pad[:, 0, :], 1.0)
        nc.gpsimd.memset(t_pad[:, 0, :], 1.0)
        nc.gpsimd.memset(sel[:], 0.0)
        nc.vector.tensor_copy(out=gz_f[:], in_=gz_col[:])

        def put(eng, dst, src):
            if eng is nc.vector:
                nc.vector.tensor_copy(out=dst, in_=src)
            else:
                nc.scalar.copy(out=dst, in_=src)

        def mat(c):
            for dst, src in mat_sources(c):
                put(MATS[c], dst, src)

        def consts(i):
            nc.vector.tensor_scalar(out=tg[i][:, 0, :], in0=ones[:], scalar1=gz_f[:, 0:1], scalar2=None, op0=ALU.mult)

        def pads():
            put(PADT, t_pad[:, 1:4, :], t_nat[:].rearrange("p q c -> p c q"))
            put(PADT, v_pad[:, 1:8, :], v_nat[:].rearrange("p q c -> p c q"))
            put(PADS, a_pad[:, 1:16, :], a_nat[:].rearrange("p q c -> p c q"))

        def small():
            nc.gpsimd.tensor_scalar(out=sgn01[:], in0=gh_col[:], scalar1=0.0, scalar2=None, op0=ALU.is_ge)
            nc.gpsimd.tensor_scalar(out=sgn[:], in0=sgn01[:], scalar1=2.0, scalar2=-1.0, op0=ALU.mult, op1=ALU.add)
            nc.gpsimd.tensor_tensor(out=gh_abs[:], in0=gh_col[:], in1=sgn[:], op=ALU.mult)
            for k in range(4):
                nc.gpsimd.tensor_scalar(
                    out=sel[32 * k : 32 * k + 1, k, :],
                    in0=gz_row[32 * k : 32 * k + 1, :].rearrange("o (p j) -> o j p", j=4)[:, k, :],
                    scalar1=1.0, scalar2=0.0, op0=ALU.mult, op1=ALU.add,
                )

        av_tiles = {}
        y_tiles = []
        hp_tiles = {}
        pieces = {}
        p1_tiles = {}

        early_ps = {}

        def early_turn(c):
            a_ps = psum.tile([P, QC, P], BF16, name="a_ps", tag="p", bufs=PB)
            v_ps = psum.tile([P, QC, P], BF16, name="v_ps", tag="o", bufs=2)
            for j in range(QC):
                nc.tensor.transpose(v_ps[:, j, :], v_mats[c][:, j].rearrange("p i s -> p (i s)"), ident[:])
            for j in range(QC):
                nc.tensor.transpose(a_ps[:, j, :], a_mats[c][:, j].rearrange("p i s -> p (i s)"), ident[:])
            v_sb = work.tile([P, CW], BF16, name="v_sb", tag="v_sb", bufs=2)
            if c == 0:
                nc.vector.tensor_copy(out=v_sb[:], in_=v_ps[:].rearrange("p q h -> p (q h)"))
            else:
                nc.scalar.copy(out=v_sb[:], in_=v_ps[:].rearrange("p q h -> p (q h)"))
            early_ps[c] = (a_ps, v_sb)

        def early_mul(c):
            a_ps, v_sb = early_ps[c]
            av = work.tile([P, CW], F32, name="av", tag="av", bufs=AVB)
            nc.vector.tensor_tensor(out=av[:], in0=a_ps[:].rearrange("p q h -> p (q h)"), in1=v_sb[:], op=ALU.mult)
            av_tiles[c] = av

        def late_factors(c):
            ar, vr, r, base = pieces[c]
            lo = c * CW - base
            av = work.tile([P, CW], F32, name="av", tag="av", bufs=AVB)
            (nc.vector if c < GAV else nc.gpsimd).tensor_tensor(out=av[:], in0=ar[:, lo : lo + CW], in1=vr[:, lo : lo + CW], op=ALU.mult)
            av_tiles[c] = av

        def t_planes(c):
            tb0 = psum.tile([P, 2, CW], BF16, name="tb0", tag="y0", bufs=1)
            tb1 = psum.tile([P, CW], BF16, name="tb1", tag="y1", bufs=1)
            for k in range(DT):
                for j in range(QC):
                    q = QC * c + j
                    dst = tb0[:, k, j * P : (j + 1) * P] if k < 2 else tb1[:, j * P : (j + 1) * P]
                    nc.tensor.transpose(dst, t_nat[:, q, k : k + 1].to_broadcast([P, P]), ident[:])
            for k in range(DT):
                src = tb0[:, k, :] if k < 2 else tb1[:]
                nc.scalar.activation(out=tg[c % 2][:, k + 1, :], in_=src, func=ACT.Copy, scale=gz_f[:, k + 1 : k + 2])

        def y_block(c, j):
            ar, vr, r, base = pieces[c]
            lo = c * CW - base + j * P
            y = y_tiles[(QC * c + j) % YB]
            for k in range(1, 4):
                nc.tensor.matmul(y[:, k, :], lhsT=sel[:, k, :], rhs=r[:, lo : lo + P], start=True, stop=True)

        def fuse(c, j, jn=1):
            zg = qin(c + 1)[:, 0:CW, :]
            cols = slice(j * P, (j + jn) * P)
            x = av_tiles[c][:, cols].unsqueeze(2).to_broadcast([P, jn * P, 4])
            if c < CTYPE:
                y = tg[c % 2][:, :, cols]
            else:
                y = y_tiles[(QC * c + j) % YB][:]
            nc.vector.tensor_tensor(out=zg[:, cols, :], in0=y.rearrange("p k n -> p n k"), in1=x, op=ALU.mult)

        q_tiles = {}
        c_tiles = {}

        def qin(r):
            if r not in q_tiles:
                qt = work.tile([P, 2 * CW, 4], BF16, name="qt", tag="qt", bufs=QB, align_bytes=64)
                q_tiles[r] = qt
            return q_tiles[r]

        def quant(r, lo, hi):
            if r not in c_tiles:
                qc = work.tile([P, 2 * CW], U32, name="qc", tag="qc", bufs=CB, align_bytes=64)
                qs = work.tile([P, 2 * CW], U8, name="qs", tag="qs", bufs=CB, align_bytes=64)
                c_tiles[r] = (qc, qs)
            qc, qs = c_tiles[r]
            nc.vector.quantize_mx(out=qc[:, lo:hi].bitcast(FP8X4), scales=qs[:, lo:hi], in_=qin(r)[:, lo:hi, :].rearrange("p n k -> p (n k)"))

        def stage1(c, ks, vec_ks=()):
            zc, zs = c_tiles[c + 1]
            if c not in hp_tiles:
                hp = work.tile([P, 4, CW], BF16, name="hp", tag="hp", bufs=HB)
                hp_tiles[c] = hp
            hp = hp_tiles[c]
            for k in ks:
                p1 = psum.tile([P, CW], F32, name="p1", tag="p", bufs=PB)
                nc.tensor.matmul_mx(
                    out=p1[:],
                    lhsT=w1_codes[:, k * P : (k + 1) * P].bitcast(FP8X4),
                    lhsT_scale=w1_scales[:, k * P : (k + 1) * P],
                    rhs=zc[:, 0:CW].bitcast(FP8X4),
                    rhs_scale=zs[:, 0:CW],
                    start=True,
                    stop=True,
                )
                p1_tiles[c, k] = p1
                if k not in vec_ks:
                    nc.scalar.activation(out=hp[:, k, :], in_=p1[:], func=ACT.Relu, scale=gh_abs[:, k : k + 1])

        def relu_v(c, k):
            nc.vector.tensor_scalar(out=hp_tiles[c][:, k, :], in0=p1_tiles[c, k][:], scalar1=0.0, scalar2=gh_abs[:, k : k + 1],
                                    op0=ALU.max, op1=ALU.mult)

        def interleave(eng, c, lo, hi):
            dst = qin(c + LQ)[:, CW + lo : CW + hi, :].rearrange("p (c i) k -> p c k i", i=4)
            src = hp_tiles[c][:, :, lo:hi].rearrange("p k (c i) -> p c k i", i=4)
            if eng == "g":
                g_copy(dst, src)
            elif eng == "v":
                nc.vector.tensor_copy(out=dst, in_=src)
            else:
                nc.scalar.copy(out=dst, in_=src)

        out_v = out.rearrange("(h q) o -> h q o", q=QS)
        o_tiles = {}

        def stage2(c, jj, vec=False, store=None):
            hc, hs = c_tiles[c + LQ]
            if c not in o_tiles:
                osb = work.tile([P, QC, O], F32, name="osb", tag="osb", bufs=4)
                o_tiles[c] = osb
            osb = o_tiles[c]
            po = psum.tile([P, 2, O], F32, name="po", tag="o", bufs=2)
            for j in range(2):
                cols = slice(CW + (2 * jj + j) * P, CW + (2 * jj + j + 1) * P)
                nc.tensor.matmul_mx(
                    out=po[:, j, :],
                    lhsT=hc[:, cols].bitcast(FP8X4),
                    lhsT_scale=hs[:, cols],
                    rhs=w2_codes[:].bitcast(FP8X4),
                    rhs_scale=w2_scales[:],
                    start=True,
                    stop=True,
                )
            if vec:
                nc.vector.tensor_copy(out=osb[:, 2 * jj : 2 * jj + 2, :], in_=po[:])
            else:
                nc.scalar.copy(out=osb[:, 2 * jj : 2 * jj + 2, :], in_=po[:])
            if store is not None:
                nc.sync.dma_start(out=out_v[:, QC * c + store[0] : QC * c + store[1], :], in_=osb[:, store[0] : store[1], :])

        mat(0)
        consts(0)
        t_planes(0)
        early_turn(0)
        early_mul(0)
        def bounce():
            turned = keep.tile([P, 14, P], BF16)
            src_cols = [a_pad[:].rearrange("p c q -> p (c q)"), v_pad[:].rearrange("p c q -> p (c q)"), t_pad[:].rearrange("p c q -> p (c q)")]
            m = 0
            for cols_ap, cnt in ((src_cols[0], 4), (src_cols[0], 4), (src_cols[1], 4), (src_cols[2], 2)):
                first = 4 if m == 4 else 0
                tp = psum.tile([P, 4, P], BF16, name="tp", tag="p", bufs=PB)
                for i in range(cnt):
                    nc.tensor.transpose(tp[:, i, :], cols_ap[:, (first + i) * P : (first + i + 1) * P], ident[:])
                nc.scalar.copy(out=turned[:, m : m + cnt, :], in_=tp[:, 0:cnt, :])
                m += cnt
            park_rows = 14 * P * P // 2 // O
            park = out[N - park_rows : N, :].rearrange("r o -> (r o)").bitcast(BF16)
            nc.sync.dma_start(out=park.rearrange("(m p h) -> p m h", p=P, h=P), in_=turned[:])
            for c0, c1 in ((3, 4), (4, 8), (8, 16)):
                n0, n1 = c0 * CW, c1 * CW
                w = n1 - n0
                ar = keep.tile([P, w], BF16, name="ar%d" % c0)
                vr = keep.tile([P, w], BF16, name="vr%d" % c0)
                r = keep.tile([P, w], BF16, name="r%d" % c0)
                if c0 >= CTYPE:
                    nc.sync.dma_start(out=r[:], in_=park[24 * N : 28 * N].rearrange("(k n) -> k n", k=4)[:, n0:n1].unsqueeze(1).to_broadcast([4, 32, w]))
                nc.sync.dma_start(out=ar[:], in_=park[0 : 16 * N].rearrange("(i n) -> i n", i=16)[:, n0:n1].unsqueeze(1).to_broadcast([16, 8, w]))
                nc.sync.dma_start(out=vr[:], in_=park[16 * N : 24 * N].rearrange("(j n) -> j n", j=8)[:, n0:n1].unsqueeze(0).to_broadcast([16, 8, w]))
                for c in range(c0, c1):
                    pieces[c] = (ar, vr, r, n0)

        w1_wide = keep.tile([P, 4, H], BF16)
        w1_grp = keep.tile([P, H, 4], BF16, align_bytes=64)
        w1_codes = keep.tile([P, H], U32, align_bytes=64)
        w1_scales = keep.tile([P, H], U8, align_bytes=64)
        w2_grp = keep.tile([P, O, 4], BF16, align_bytes=64)
        w2_codes = keep.tile([P, O], U32, align_bytes=64)
        w2_scales = keep.tile([P, O], U8, align_bytes=64)

        def weights_s(ks):
            for k in ks:
                nc.scalar.activation(out=w1_wide[:, k, :], in_=w1_raw[:, k, :].bitcast(FP8), func=ACT.Copy, scale=w1_sc[:, k : k + 1])

        def weights_w2():
            nc.vector.tensor_tensor(
                out=w2_grp[:],
                in0=w2_raw[:].rearrange("p j n -> p n j"),
                in1=sgn[:].unsqueeze(1).to_broadcast([P, O, 4]),
                op=ALU.mult,
            )

        def weights_w1():
            nc.vector.tensor_copy(out=w1_grp[:].rearrange("p (k m) j -> p k m j", k=4), in_=w1_wide[:].rearrange("p j (m k) -> p k m j", k=4))

        def weights_q():
            nc.vector.quantize_mx(out=w2_codes[:].bitcast(FP8X4), scales=w2_scales[:], in_=w2_grp[:].rearrange("p n j -> p (n j)"))
            nc.vector.quantize_mx(out=w1_codes[:].bitcast(FP8X4), scales=w1_scales[:], in_=w1_grp[:].rearrange("p n j -> p (n j)"))

        for r in range(NCH):
            if r >= 1:
                fuse(r - 1, 3)
            if r < CTYPE:
                fuse(r, 0, 3)
            else:
                for j in range(3):
                    fuse(r, j)
            if r == 0:
                mat(1)
                early_turn(1)
                early_mul(1)
                consts(1)
                t_planes(1)
                pads()
                small()
                weights_s((0, 1, 2, 3))
                weights_w2()
                bounce()
                mat(2)
                early_turn(2)
            else:
                if EARLY <= r + 1 < NCH:
                    late_factors(r + 1)
                if r + 1 < CTYPE:
                    t_planes(r + 1)
            if r == 1:
                weights_w1()
            if r == CTYPE - 1:
                for i in range(YB):
                    y = psum.tile([P, 4, P], F32, name="y%d" % i, tag="y%d" % i, bufs=1)
                    nc.tensor.matmul(y[:, 0, :], lhsT=sel[:, 0, :], rhs=pieces[CTYPE][2][:, 0:P], start=True, stop=True)
                    y_tiles.append(y)
            if CTYPE <= r:
                y_block(r, 3)
            if CTYPE <= r + 1 < NCH:
                for j in range(3):
                    y_block(r + 1, j)
            if 0 <= r - LI < NCH - 3:
                interleave("s", r - LI, ILV, CW)
            if r >= 1:
                quant(r, 0, 2 * CW if r >= LQ else CW)
                if r == 1:
                    weights_q()
                stage1(r - 1, range(4))
            if 0 <= r - LQ:
                stage2(r - LQ, 0)
                stage2(r - LQ, 1, store=(0, 4))
            if 0 <= r - LI < NCH - 3:
                interleave("v", r - LI, ILG, ILV)
            if r == 1:
                early_mul(2)
        last = NCH - 1
        fuse(last, 3)
        quant(NCH, 0, 2 * CW)
        stage1(last, (0, 1, 2), (2,))
        stage2(last - 3, 0)
        stage2(last - 3, 1, store=(0, 4))
        stage1(last, (3,), (3,))
        interleave("v", last - 2, 0, 512)
        interleave("v", last - 1, 0, 512)
        quant(NCH + 1, CW, 2 * CW)
        stage2(last - 2, 0)
        relu_v(last, 2)
        relu_v(last, 3)
        quant(NCH + 2, CW, 2 * CW)
        stage2(last - 2, 1, store=(0, 4))
        stage2(last - 1, 0)
        stage2(last - 1, 1, store=(0, 4))
        interleave("v", last, 0, 256)
        interleave("v", last, 256, 512)
        quant(NCH + 3, CW, CW + 256)
        stage2(last, 0, store=(0, 2))
        quant(NCH + 3, CW + 256, 2 * CW)
        stage2(last, 1, vec=True, store=(2, 4))
